import numpy as np
import ml_dtypes


def mxq(x, axis, fmt="e4m3"):
    dtype, down = {"e4m3": (ml_dtypes.float8_e4m3fn, 7), "e5m2": (ml_dtypes.float8_e5m2, 14)}[fmt]
    v = np.moveaxis(np.asarray(x, np.float32).astype(ml_dtypes.bfloat16).astype(np.float64), axis, -1)
    blocks = v.reshape(v.shape[:-1] + (-1, 32))
    amax = np.abs(blocks).max(-1, keepdims=True)
    byte = np.maximum(np.where(amax > 0, np.frexp(amax)[1] - 1 + 127, 0) - down, 1)
    scale = np.exp2(byte - 127.0)
    codes = (blocks / scale).astype(np.float32).astype(dtype).astype(np.float64)
    return np.moveaxis((codes * scale).reshape(v.shape), -1, axis)


WIDE = False


def mx_kscale(k):
    if not WIDE:
        return np.ones(k)
    levels = np.array([10, -10, 5, -5, 0])
    if k % 512:
        return np.exp2(np.random.permutation(np.resize(levels, k // 32))).repeat(32)
    a = np.empty((k // 512, 16))
    for p in range(k // 512):
        a[p, :8] = np.random.permutation(np.resize(levels, 8))
        for g in range(8):
            far = levels[np.abs(levels - a[p, g]) >= 10]
            a[p, g + 8] = far[np.random.randint(len(far))]
    return np.exp2(a.ravel()).repeat(32)


BF16 = ml_dtypes.bfloat16


def bf(x):
    return np.asarray(x, np.float32).astype(BF16)


def f64(x):
    return np.asarray(x).astype(np.float64)


E2M1 = np.array([0.0, 0.5, 1.0, 1.5, 2.0, 3.0, 4.0, 6.0, -0.0, -0.5, -1.0, -1.5, -2.0, -3.0, -4.0, -6.0])


def pack_weight(w, fmt):
    k, n = w.shape
    w = f64(bf(w)).reshape(k // 32, 32, n)
    amax = np.abs(w).max(1)
    if fmt == "e4m3":
        byte = np.frexp(amax)[1] - 1 + 127 - 7
    else:
        mant, ex = np.frexp(amax / 6.0)
        byte = np.where(mant > 0.5, ex, ex - 1) + 127
    byte = np.clip(np.where(amax > 0, byte, 1), 1, 254)
    scaled = (w * np.exp2(127.0 - byte)[:, None, :]).reshape(k, n).astype(np.float32)
    by_word = np.ascontiguousarray(scaled.reshape(k // 512, 128, 4, n).transpose(0, 1, 3, 2))
    if fmt == "e4m3":
        words = by_word.astype(ml_dtypes.float8_e4m3fn).view(np.uint8)
    else:
        c = by_word.astype(ml_dtypes.float4_e2m1fn).view(np.uint8) & 0xF
        words = c[..., 0::2] | (c[..., 1::2] << 4)
    return np.ascontiguousarray(words), np.ascontiguousarray(byte.astype(np.uint8).reshape(k // 512, 16, n))


def unpack_weight(words, scales, fmt):
    g, p, n, _ = words.shape
    if fmt == "e4m3":
        vals = np.ascontiguousarray(words).view(ml_dtypes.float8_e4m3fn).astype(np.float64)
    else:
        nib = np.empty((g, p, n, 4), np.uint8)
        nib[..., 0::2] = words & 0xF
        nib[..., 1::2] = words >> 4
        vals = E2M1[nib]
    vals = vals * np.repeat(np.exp2(scales.astype(np.float64) - 127.0), 8, axis=1)[..., None]
    return vals.transpose(0, 1, 3, 2).reshape(g * 512, n)
def pack4(w):
    words, scales = pack_weight(w, "e2m1")
    return words.reshape(words.shape[0], 128, -1), scales


def unpack4(words, scales):
    return unpack_weight(words.reshape(words.shape[0], 128, -1, 2), scales, "e2m1")


H, J, D, K, C = 2048, 1024, 512, 1024, 512

USTD = 0.5
LSTD = 0.3


def draw0():
    s1, s2, s3 = mx_kscale(D), mx_kscale(K), mx_kscale(H)
    z = np.random.standard_normal((H, D)) * s1
    w = USTD * np.random.standard_normal((D, J)) / np.sqrt(D) / s1[:, None]
    x = np.random.standard_normal((H, K)) * s2
    v = USTD * np.random.standard_normal((K, J)) / np.sqrt(K) / s2[:, None]
    a = np.exp(LSTD * np.random.standard_normal(H)) * s3
    y = np.random.standard_normal((H, C)) / np.sqrt(H) / s3[:, None]
    size = np.exp(LSTD * np.random.standard_normal(J))
    v_words, v_scales = pack4(v)
    y_words, y_scales = pack4(y)
    return {"z": bf(z), "w": bf(w), "x": bf(x),
            "v_words": v_words, "v_scales": v_scales,
            "a": bf(a), "size": bf(size),
            "y_words": y_words, "y_scales": y_scales}


def core(z, w, x, v_words, v_scales, a, size, y_words, y_scales):
    travel = mxq(f64(z), 1, "e4m3") @ mxq(f64(w), 0, "e4m3")
    taste = mxq(f64(x), 1, "e4m3") @ unpack4(v_words, v_scales)
    patronage = np.exp(travel + taste) * f64(a)[:, None]
    flows = mxq(patronage, 0, "e4m3").T @ unpack4(y_words, y_scales)
    return flows * f64(size)[:, None]


def e4m3fn_bytes(y):
    return np.clip(np.asarray(y, np.float64), -448.0, 448.0).astype(np.float32).astype(ml_dtypes.float8_e4m3fn).view(np.uint8)


def e4m3fn_values(b):
    return np.asarray(b, np.uint8).view(ml_dtypes.float8_e4m3fn).astype(np.float64)


def setup_inputs():
    d = draw0()
    x0 = np.asarray(d['x']).astype(np.float64)
    s = (np.max(np.abs(x0), axis=(0,), keepdims=True) / 448.0).astype(np.float32)
    out = {}
    for k, v in d.items():
        if k == 'x':
            out['x_bytes'] = e4m3fn_bytes(x0 / s.astype(np.float64))
            out['x_scale'] = s
        else:
            out[k] = v
    return out


def reference(z, w, x_bytes, x_scale, v_words, v_scales, a, size, y_words, y_scales):
    return core(z, w, e4m3fn_values(x_bytes) * x_scale.astype(np.float64), v_words, v_scales, a, size, y_words, y_scales)

@@ -1,0 +1,385 @@
+from contextlib import ExitStack
+
+import concourse.mybir as mybir
+from concourse.masks import make_identity
+
+H, J, D, K, C = 2048, 1024, 512, 1024, 512
+FLOPS = 2 * H * J * (D + K) + 2 * J * C * H
+
+F32 = mybir.dt.float32
+BF16 = mybir.dt.bfloat16
+U32 = mybir.dt.uint32
+I32 = mybir.dt.int32
+U8 = mybir.dt.uint8
+FP8 = mybir.dt.float8_e4m3fn
+FP8X4 = mybir.dt.float8_e4m3fn_x4
+FP4X4 = mybir.dt.float4_e2m1fn_x4
+ACT = mybir.ActivationFunctionType
+ALU = mybir.AluOpType
+
+P = 128
+G = H // 512
+NT = 4 * G
+HALF = J // 2
+
+
+def tile_huff_retail_flows_s3_kernel(
+    tc, z, w, x_bytes, x_scale, v_words, v_scales, a, size, y_words, y_scales, out
+):
+    nc = tc.nc
+    with ExitStack() as ctx:
+        keep = ctx.enter_context(tc.tile_pool(name="keep", bufs=1))
+        work = ctx.enter_context(tc.tile_pool(name="work", bufs=2))
+        psum = ctx.enter_context(tc.psum_pool(name="psum", bufs=1))
+        ctx.enter_context(tc.manual_schedule())
+
+        def kept(name, shape, dtype):
+            return keep.tile(shape, dtype, name=name, tag=name, align_bytes=64)
+
+        def bank(kind):
+            return psum.tile([P, 512], F32, name="bank_" + kind, tag=kind, bufs=3 if kind == "t" else 5)
+
+        ident = kept("ident", [P, P], F32)
+        warm = kept("warm", [P, 1], F32)
+        warm_out = kept("warm_out", [P, 1], F32)
+        a_in = kept("a_in", [P, G, 4], BF16)
+        ln_a = kept("ln_a", [P, NT], F32)
+        xs_cols = kept("xs_cols", [P, 8], F32)
+        xs_wide = kept("xs_wide", [P, K], F32)
+        size_rows = kept("size_rows", [P, P], BF16)
+        size_rows32 = kept("size_rows32", [P, P], F32)
+        size_cols = kept("size_cols", [P, 8], F32)
+        v_sb = kept("v_sb", [P, 2, 2 * J], U8)
+        v_sc = kept("v_sc", [P, 2 * J], U8)
+        y_sb = kept("y_sb", [P, G, 2 * C], U8)
+        y_sc = kept("y_sc", [P, G * C], U8)
+        w_raw = [kept("w_raw%d" % h, [P, 4, HALF], BF16) for h in range(2)]
+        w_grp = [kept("w_grp%d" % h, [P, HALF, 4], BF16) for h in range(2)]
+        w_q = [kept("w_q%d" % h, [P, HALF], U32) for h in range(2)]
+        w_s = [kept("w_s%d" % h, [P, HALF], U8) for h in range(2)]
+        z_raw = [kept("z_raw%d" % g, [P, 4, D], BF16) for g in range(G)]
+        z_q = [kept("z_q%d" % g, [P, 512], U32) for g in range(G)]
+        z_s = [kept("z_s%d" % g, [P, 512], U8) for g in range(G)]
+        x_raw = [kept("x_raw%d" % g, [P, 4 * K], U8) for g in range(G)]
+        x_q = [kept("x_q%d" % i, [P, 2, P], U32) for i in range(NT)]
+        x_s = [kept("x_s%d" % i, [P, 2, P], U8) for i in range(NT)]
+        p_q = [[kept("p_q%d_%d" % (g, h), [P, HALF], U32) for h in range(2)] for g in range(G)]
+        p_s = [[kept("p_s%d_%d" % (g, h), [P, HALF], U8) for h in range(2)] for g in range(G)]
+        z_grp = {}
+        x_bf = {}
+        x_grp = {}
+        p_raw = {}
+        p_grp = {}
+
+        nc.scalar.dma_start(out=a_in[:], in_=a.rearrange("(g p t) -> p g t", p=P, t=4))
+        nc.sync.dma_start(out=xs_cols[:], in_=x_scale.rearrange("o (p c) -> p (o c)", c=8))
+
+        w_view = w.rearrange("(p t) j -> p t j", t=4)
+
+        def load_w(h):
+            nc.sync.dma_start(out=w_raw[h][:], in_=w_view[:, :, h * HALF : (h + 1) * HALF])
+
+        def load_z(g):
+            nc.sync.dma_start(out=z_raw[g][:], in_=z[512 * g : 512 * (g + 1), :].rearrange("(p t) k -> p t k", t=4))
+
+        def load_x(g):
+            nc.sync.dma_start(
+                out=x_raw[g][:], in_=x_bytes[512 * g : 512 * (g + 1), :].rearrange("(p t) k -> p (t k)", t=4)
+            )
+
+        def load_scales(tile, src, groups):
+            for r in range(4):
+                nc.sync.dma_start(
+                    out=tile[r:P:32, :].bitcast(I32).rearrange("q (g n) -> q g n", g=groups),
+                    in_=src.bitcast(I32).rearrange("g (q r) n -> r q g n", r=4)[r],
+                )
+
+        nc.vector.memset(warm[:], 1.0)
+        nc.vector.memset(v_sc[:].bitcast(I32), 0)
+        nc.vector.memset(y_sc[:].bitcast(I32), 0)
+        make_identity(nc, ident[:])
+        nc.gpsimd.memset(size_rows[:], 0.0)
+        nc.gpsimd.dma_start(out=size_rows[0:8, :], in_=size.rearrange("(c p) -> c p", p=P))
+        nc.gpsimd.tensor_copy(out=size_rows32[:], in_=size_rows[:])
+
+        load_w(0)
+        load_z(0)
+        load_x(0)
+        load_scales(v_sc, v_scales, 2)
+        nc.sync.dma_start(out=v_sb[:], in_=v_words.rearrange("g p n -> p g n"))
+        load_w(1)
+        load_x(1)
+        load_z(1)
+        load_x(2)
+        load_z(2)
+        load_x(3)
+        load_z(3)
+        load_scales(y_sc, y_scales, G)
+        nc.sync.dma_start(out=y_sb[:], in_=y_words.rearrange("g p n -> p g n"))
+
+        def widen(i):
+            x_bf[i] = work.tile([P, K], BF16, name="x_bf", tag="x_bf", bufs=5, align_bytes=64)
+            t = i % 4
+            nc.vector.tensor_tensor(
+                out=x_bf[i][:],
+                in0=x_raw[i // 4][:, t * K : (t + 1) * K].bitcast(FP8),
+                in1=xs_wide[:],
+                op=ALU.mult,
+            )
+
+        def turn_x(i):
+            b = bank("t")
+            words = x_bf[i][:].bitcast(F32)
+            for kg in range(2):
+                for u in range(2):
+                    c = 2 * kg + u
+                    nc.tensor.transpose(
+                        b[:, c * P : (c + 1) * P], words[:, 256 * kg + u : 256 * (kg + 1) : 2], ident[:]
+                    )
+            return b
+
+        def copy_out(engine, dst, src):
+            if engine == "s":
+                nc.scalar.copy(out=dst, in_=src)
+            else:
+                nc.vector.tensor_copy(out=dst, in_=src)
+
+        def empty_x(i, b, engine):
+            x_grp[i] = work.tile([P, 8 * P], BF16, name="x_grp", tag="x_grp", bufs=3, align_bytes=64)
+            dst = x_grp[i][:].bitcast(F32).rearrange("p (k h u) -> p k h u", k=2, u=2)
+            copy_out(engine, dst, b[:].rearrange("p (k u h) -> p k h u", k=2, u=2))
+
+        def quant_x(i):
+            nc.vector.quantize_mx(
+                out=x_q[i][:].rearrange("p k h -> p (k h)").bitcast(FP8X4),
+                scales=x_s[i][:].rearrange("p k h -> p (k h)"),
+                in_=x_grp[i][:],
+            )
+
+        def turn_z(g, half):
+            b = bank("t")
+            for j in range(2):
+                t = 2 * half + j
+                words = z_raw[g][:, t, :].bitcast(F32)
+                for u in range(2):
+                    c = 2 * j + u
+                    nc.tensor.transpose(b[:, c * P : (c + 1) * P], words[:, u:256:2], ident[:])
+            return b
+
+        def empty_z(g, half, b, engine):
+            if half == 0:
+                z_grp[g] = work.tile([P, 16 * P], BF16, name="z_grp", tag="z_grp", bufs=2, align_bytes=64)
+            dst = z_grp[g][:].bitcast(F32).rearrange("p (s t h u) -> p s t h u", s=2, t=2, u=2)[:, half]
+            copy_out(engine, dst, b[:].rearrange("p (t u h) -> p t h u", t=2, u=2))
+
+        def quant_z(g):
+            nc.vector.quantize_mx(out=z_q[g][:].bitcast(FP8X4), scales=z_s[g][:], in_=z_grp[g][:])
+
+        def group4(engine, dst, src):
+            copy_out(
+                engine, dst.rearrange("p (c i) t -> p c t i", i=4), src.rearrange("p t (c i) -> p c t i", i=4)
+            )
+
+        def quant_w(h):
+            nc.vector.quantize_mx(
+                out=w_q[h][:].bitcast(FP8X4), scales=w_s[h][:], in_=w_grp[h][:].rearrange("p n t -> p (n t)")
+            )
+
+        u_bank = {}
+
+        def u_pass(i, h, which):
+            if which == 0:
+                u_bank[i, h] = bank("u")
+            g, t = divmod(i, 4)
+            cols = slice(t * P, (t + 1) * P)
+            if which == 0:
+                lhs, lsc = z_q[g][:, cols].bitcast(FP8X4), z_s[g][:, cols]
+                rhs, rsc = w_q[h][:].bitcast(FP8X4), w_s[h][:]
+            else:
+                kg = which - 1
+                lhs, lsc = x_q[i][:, kg, :].bitcast(FP8X4), x_s[i][:, kg, :]
+                rhs = v_sb[:, kg, 2 * HALF * h : 2 * HALF * (h + 1)].bitcast(FP4X4)
+                rsc = v_sc[:, J * kg + HALF * h : J * kg + HALF * (h + 1)]
+            nc.tensor.matmul_mx(
+                out=u_bank[i, h][:], lhsT=lhs, lhsT_scale=lsc, rhs=rhs, rhs_scale=rsc,
+                start=(which == 0), stop=(which == 2),
+            )
+
+        def u_group(i, h):
+            for which in range(3):
+                u_pass(i, h, which)
+
+        def attract(i, h):
+            g, t = divmod(i, 4)
+            if t == 0:
+                p_raw[g, h] = work.tile([P, 4, HALF], BF16, name="p_raw", tag="p_raw", bufs=5, align_bytes=64)
+            nc.scalar.activation(
+                out=p_raw[g, h][:, t, :], in_=u_bank[i, h][:], func=ACT.Exp, bias=ln_a[:, i : i + 1], scale=1.0
+            )
+
+        def group_p(g, h):
+            p_grp[g, h] = work.tile([P, HALF, 4], BF16, name="p_grp", tag="p_grp", bufs=2, align_bytes=64)
+            group4("v", p_grp[g, h][:], p_raw[g, h][:])
+
+        def quant_p(g, h):
+            nc.vector.quantize_mx(
+                out=p_q[g][h][:].bitcast(FP8X4), scales=p_s[g][h][:],
+                in_=p_grp[g, h][:].rearrange("p n t -> p (n t)"),
+            )
+
+        f_bank = {}
+
+        def f_pass(jt, g):
+            if g == 0:
+                f_bank[jt] = bank("t" if jt < 3 else "u")
+            h, c = divmod(jt, 4)
+            cols = slice(c * P, (c + 1) * P)
+            nc.tensor.matmul_mx(
+                out=f_bank[jt][:],
+                lhsT=p_q[g][h][:, cols].bitcast(FP8X4), lhsT_scale=p_s[g][h][:, cols],
+                rhs=y_sb[:, g, :].bitcast(FP4X4), rhs_scale=y_sc[:, C * g : C * (g + 1)],
+                start=(g == 0), stop=(g == G - 1),
+            )
+
+        def finish(jt, engine, c0, c1):
+            o = work.tile([P, c1 - c0], F32, name="o_sb", tag="o_sb%d" % (c1 - c0), bufs=4, align_bytes=64)
+            if engine == "s":
+                nc.scalar.activation(
+                    out=o[:], in_=f_bank[jt][:, c0:c1], func=ACT.Copy, scale=size_cols[:, jt : jt + 1]
+                )
+            else:
+                nc.vector.tensor_scalar(
+                    out=o[:], in0=f_bank[jt][:, c0:c1], scalar1=size_cols[:, jt : jt + 1], scalar2=None, op0=ALU.mult
+                )
+            nc.sync.dma_start(out=out[jt * P : (jt + 1) * P, c0:c1], in_=o[:])
+
+        nc.scalar.activation(out=warm_out[:], in_=warm[:], func=ACT.Ln)
+        nc.scalar.activation(out=ln_a[:], in_=a_in[:].rearrange("p g t -> p (g t)"), func=ACT.Ln)
+        nc.scalar.activation(out=warm_out[:], in_=warm[:], func=ACT.Exp)
+
+        sc_banks = [bank("u"), bank("u")]
+        for c in range(8):
+            nc.tensor.transpose(
+                sc_banks[c // 4][:, (c % 4) * P : (c % 4 + 1) * P],
+                xs_cols[:, c : c + 1].to_broadcast([P, P]),
+                ident[:],
+            )
+        for i in range(2):
+            copy_out(
+                "vs"[i],
+                xs_wide[:].rearrange("p (n c) -> p n c", c=8)[:, :, 4 * i : 4 * i + 4],
+                sc_banks[i][:].rearrange("p (c n) -> p n c", c=4),
+            )
+        size_bank = bank("u")
+        nc.tensor.transpose(size_bank[:, 0:P], size_rows32[:], ident[:])
+        group4("v", w_grp[0][:], w_raw[0][:])
+        zb = [turn_z(0, 0), turn_z(0, 1)]
+        empty_z(0, 0, zb[0], "s")
+        empty_z(0, 1, zb[1], "s")
+        quant_w(0)
+        widen(0)
+        quant_z(0)
+        b0 = turn_x(0)
+        empty_x(0, b0, "s")
+        widen(1)
+        b1 = turn_x(1)
+        for c in range(2):
+            cs = slice(c * 256, (c + 1) * 256)
+            group4("s", w_grp[1][:, cs, :], w_raw[1][:, :, cs])
+            if c == 0:
+                empty_x(1, b1, "s")
+        quant_x(0)
+        u_pass(0, 0, 0)
+        u_pass(1, 0, 0)
+        u_pass(0, 0, 1)
+        u_pass(0, 0, 2)
+        attract(0, 0)
+        widen(2)
+        quant_x(1)
+        u_pass(1, 0, 1)
+        u_pass(1, 0, 2)
+        attract(1, 0)
+        quant_w(1)
+        u_group(0, 1)
+        attract(0, 1)
+        u_group(1, 1)
+        attract(1, 1)
+        widen(3)
+        nc.vector.tensor_copy(out=size_cols[:], in_=size_bank[:, 0:8])
+
+        p_work = {}
+        for g in range(3):
+            p_work[2 * g + 2] = (g, 0)
+            p_work[2 * g + 3] = (g, 1)
+        for n in range(0, 8):
+            nxt = n + 1
+            banks = []
+            if nxt < 8:
+                banks.append((turn_x(2 * nxt), "x", 2 * nxt))
+                banks.append((turn_x(2 * nxt + 1), "x", 2 * nxt + 1))
+                gz, hz = divmod(nxt + 1, 2)
+                if gz < G:
+                    banks.append((turn_z(gz, hz), "z", (gz, hz)))
+            groups = [] if n == 0 else [(2 * n, 0), (2 * n, 1), (2 * n + 1, 0), (2 * n + 1, 1)]
+            if n == 7:
+                groups = [(14, 0), (15, 0), (14, 1), (15, 1)]
+
+            def empty_one():
+                if banks:
+                    b, kind, which = banks.pop(0)
+                    if kind == "x":
+                        empty_x(which, b, "s")
+                    else:
+                        empty_z(which[0], which[1], b, "s")
+
+            if 2 * n + 4 < NT:
+                widen(2 * n + 4)
+            if n in p_work:
+                group_p(*p_work[n])
+            empty_one()
+            empty_one()
+            if nxt < 8:
+                quant_x(2 * nxt)
+            for m in range(2):
+                if m < len(groups):
+                    u_group(*groups[m])
+                    attract(*groups[m])
+                if m == 0:
+                    empty_one()
+            if 2 * n + 5 < NT:
+                widen(2 * n + 5)
+            if nxt < 8:
+                quant_x(2 * nxt + 1)
+                gz, hz = divmod(nxt + 1, 2)
+                if hz == 1 and gz < G:
+                    quant_z(gz)
+            if n in p_work:
+                quant_p(*p_work[n])
+            if n == 7:
+                u_group(*groups[2])
+                group_p(3, 0)
+                attract(*groups[2])
+                u_group(*groups[3])
+                attract(*groups[3])
+            else:
+                for m in range(2, 4):
+                    if m < len(groups):
+                        u_group(*groups[m])
+                        attract(*groups[m])
+
+        for jt in range(3):
+            for g in range(3):
+                f_pass(jt, g)
+        quant_p(3, 0)
+        group_p(3, 1)
+        for g in range(3):
+            f_pass(3, g)
+        for jt in range(4):
+            f_pass(jt, 3)
+            finish(jt, "s", 0, 512)
+        quant_p(3, 1)
+        for jt in range(4, 8):
+            for g in range(4):
+                f_pass(jt, g)
+            finish(jt, "s", 0, 256)
+            finish(jt, "v", 256, 512)

@@ -36,8 +36,8 @@ def tile_huff_retail_flows_s3_kernel(
         def kept(name, shape, dtype):
             return keep.tile(shape, dtype, name=name, tag=name, align_bytes=64)
 
-        def bank(kind):
-            return psum.tile([P, 512], F32, name="bank_" + kind, tag=kind, bufs=3 if kind == "t" else 5)
+        def bank():
+            return psum.tile([P, 512], F32, name="bank", tag="bank", bufs=8)
 
         ident = kept("ident", [P, P], F32)
         warm = kept("warm", [P, 1], F32)
@@ -58,8 +58,8 @@ def tile_huff_retail_flows_s3_kernel(
         w_q = [kept("w_q%d" % h, [P, HALF], U32) for h in range(2)]
         w_s = [kept("w_s%d" % h, [P, HALF], U8) for h in range(2)]
         z_raw = [kept("z_raw%d" % g, [P, 4, D], BF16) for g in range(G)]
-        z_q = [kept("z_q%d" % g, [P, 512], U32) for g in range(G)]
-        z_s = [kept("z_s%d" % g, [P, 512], U8) for g in range(G)]
+        z_q = [kept("z_q%d" % n, [P, 256], U32) for n in range(2 * G)]
+        z_s = [kept("z_s%d" % n, [P, 256], U8) for n in range(2 * G)]
         x_raw = [kept("x_raw%d" % g, [P, 4 * K], U8) for g in range(G)]
         x_q = [kept("x_q%d" % i, [P, 2, P], U32) for i in range(NT)]
         x_s = [kept("x_s%d" % i, [P, 2, P], U8) for i in range(NT)]
@@ -79,13 +79,17 @@ def tile_huff_retail_flows_s3_kernel(
         def load_w(h):
             nc.sync.dma_start(out=w_raw[h][:], in_=w_view[:, :, h * HALF : (h + 1) * HALF])
 
-        def load_z(g):
-            nc.sync.dma_start(out=z_raw[g][:], in_=z[512 * g : 512 * (g + 1), :].rearrange("(p t) k -> p t k", t=4))
+        def load_z(g, t0, t1):
+            src = z[512 * g : 512 * (g + 1), :].rearrange("(p t) k -> p t k", t=4)
+            nc.sync.dma_start(out=z_raw[g][:, t0:t1, :], in_=src[:, t0:t1, :])
 
-        def load_x(g):
-            nc.sync.dma_start(
-                out=x_raw[g][:], in_=x_bytes[512 * g : 512 * (g + 1), :].rearrange("(p t) k -> p (t k)", t=4)
-            )
+        def load_x(g, t0, t1):
+            src = x_bytes[512 * g : 512 * (g + 1), :].rearrange("(p t) k -> p (t k)", t=4)
+            nc.sync.dma_start(out=x_raw[g][:, t0 * K : t1 * K], in_=src[:, t0 * K : t1 * K])
+
+        def load_v(h):
+            cs = slice(2 * HALF * h, 2 * HALF * (h + 1))
+            nc.sync.dma_start(out=v_sb[:, :, cs], in_=v_words.rearrange("g p n -> p g n")[:, :, cs])
 
         def load_scales(tile, src, groups):
             for r in range(4):
@@ -102,23 +106,27 @@ def tile_huff_retail_flows_s3_kernel(
         nc.gpsimd.dma_start(out=size_rows[0:8, :], in_=size.rearrange("(c p) -> c p", p=P))
         nc.gpsimd.tensor_copy(out=size_rows32[:], in_=size_rows[:])
 
+        load_x(0, 0, 2)
         load_w(0)
-        load_z(0)
-        load_x(0)
+        load_z(0, 0, 2)
+        load_x(0, 2, 4)
+        load_z(0, 2, 4)
         load_scales(v_sc, v_scales, 2)
-        nc.sync.dma_start(out=v_sb[:], in_=v_words.rearrange("g p n -> p g n"))
+        load_v(0)
         load_w(1)
-        load_x(1)
-        load_z(1)
-        load_x(2)
-        load_z(2)
-        load_x(3)
-        load_z(3)
+        load_z(1, 0, 2)
+        load_x(1, 0, 2)
+        load_v(1)
+        load_z(1, 2, 4)
+        load_x(1, 2, 4)
+        for g in range(2, G):
+            load_z(g, 0, 4)
+            load_x(g, 0, 4)
         load_scales(y_sc, y_scales, G)
         nc.sync.dma_start(out=y_sb[:], in_=y_words.rearrange("g p n -> p g n"))
 
         def widen(i):
-            x_bf[i] = work.tile([P, K], BF16, name="x_bf", tag="x_bf", bufs=5, align_bytes=64)
+            x_bf[i] = work.tile([P, K], BF16, name="x_bf", tag="x_bf", bufs=6, align_bytes=64)
             t = i % 4
             nc.vector.tensor_tensor(
                 out=x_bf[i][:],
@@ -128,7 +136,7 @@ def tile_huff_retail_flows_s3_kernel(
             )
 
         def turn_x(i):
-            b = bank("t")
+            b = bank()
             words = x_bf[i][:].bitcast(F32)
             for kg in range(2):
                 for u in range(2):
@@ -145,7 +153,7 @@ def tile_huff_retail_flows_s3_kernel(
                 nc.vector.tensor_copy(out=dst, in_=src)
 
         def empty_x(i, b, engine):
-            x_grp[i] = work.tile([P, 8 * P], BF16, name="x_grp", tag="x_grp", bufs=3, align_bytes=64)
+            x_grp[i] = work.tile([P, 8 * P], BF16, name="x_grp", tag="x_grp", bufs=4, align_bytes=64)
             dst = x_grp[i][:].bitcast(F32).rearrange("p (k h u) -> p k h u", k=2, u=2)
             copy_out(engine, dst, b[:].rearrange("p (k u h) -> p k h u", k=2, u=2))
 
@@ -156,24 +164,23 @@ def tile_huff_retail_flows_s3_kernel(
                 in_=x_grp[i][:],
             )
 
-        def turn_z(g, half):
-            b = bank("t")
+        def turn_z(n):
+            b = bank()
+            g, half = divmod(n, 2)
             for j in range(2):
-                t = 2 * half + j
-                words = z_raw[g][:, t, :].bitcast(F32)
+                words = z_raw[g][:, 2 * half + j, :].bitcast(F32)
                 for u in range(2):
                     c = 2 * j + u
                     nc.tensor.transpose(b[:, c * P : (c + 1) * P], words[:, u:256:2], ident[:])
             return b
 
-        def empty_z(g, half, b, engine):
-            if half == 0:
-                z_grp[g] = work.tile([P, 16 * P], BF16, name="z_grp", tag="z_grp", bufs=2, align_bytes=64)
-            dst = z_grp[g][:].bitcast(F32).rearrange("p (s t h u) -> p s t h u", s=2, t=2, u=2)[:, half]
+        def empty_z(n, b, engine):
+            z_grp[n] = work.tile([P, 8 * P], BF16, name="z_grp", tag="z_grp", bufs=4, align_bytes=64)
+            dst = z_grp[n][:].bitcast(F32).rearrange("p (t h u) -> p t h u", t=2, u=2)
             copy_out(engine, dst, b[:].rearrange("p (t u h) -> p t h u", t=2, u=2))
 
-        def quant_z(g):
-            nc.vector.quantize_mx(out=z_q[g][:].bitcast(FP8X4), scales=z_s[g][:], in_=z_grp[g][:])
+        def quant_z(n):
+            nc.vector.quantize_mx(out=z_q[n][:].bitcast(FP8X4), scales=z_s[n][:], in_=z_grp[n][:])
 
         def group4(engine, dst, src):
             copy_out(
@@ -189,11 +196,11 @@ def tile_huff_retail_flows_s3_kernel(
 
         def u_pass(i, h, which):
             if which == 0:
-                u_bank[i, h] = bank("u")
-            g, t = divmod(i, 4)
+                u_bank[i, h] = bank()
+            n, t = divmod(i, 2)
             cols = slice(t * P, (t + 1) * P)
             if which == 0:
-                lhs, lsc = z_q[g][:, cols].bitcast(FP8X4), z_s[g][:, cols]
+                lhs, lsc = z_q[n][:, cols].bitcast(FP8X4), z_s[n][:, cols]
                 rhs, rsc = w_q[h][:].bitcast(FP8X4), w_s[h][:]
             else:
                 kg = which - 1
@@ -212,7 +219,7 @@ def tile_huff_retail_flows_s3_kernel(
         def attract(i, h):
             g, t = divmod(i, 4)
             if t == 0:
-                p_raw[g, h] = work.tile([P, 4, HALF], BF16, name="p_raw", tag="p_raw", bufs=5, align_bytes=64)
+                p_raw[g, h] = work.tile([P, 4, HALF], BF16, name="p_raw", tag="p_raw", bufs=6, align_bytes=64)
             nc.scalar.activation(
                 out=p_raw[g, h][:, t, :], in_=u_bank[i, h][:], func=ACT.Exp, bias=ln_a[:, i : i + 1], scale=1.0
             )
@@ -231,7 +238,7 @@ def tile_huff_retail_flows_s3_kernel(
 
         def f_pass(jt, g):
             if g == 0:
-                f_bank[jt] = bank("t" if jt < 3 else "u")
+                f_bank[jt] = bank()
             h, c = divmod(jt, 4)
             cols = slice(c * P, (c + 1) * P)
             nc.tensor.matmul_mx(
@@ -241,23 +248,27 @@ def tile_huff_retail_flows_s3_kernel(
                 start=(g == 0), stop=(g == G - 1),
             )
 
-        def finish(jt, engine, c0, c1):
-            o = work.tile([P, c1 - c0], F32, name="o_sb", tag="o_sb%d" % (c1 - c0), bufs=4, align_bytes=64)
-            if engine == "s":
-                nc.scalar.activation(
-                    out=o[:], in_=f_bank[jt][:, c0:c1], func=ACT.Copy, scale=size_cols[:, jt : jt + 1]
-                )
+        def finish(jt, split_store):
+            o = work.tile([P, C], F32, name="o_sb", tag="o_sb", bufs=8, align_bytes=64)
+            f = f_bank[jt]
+            rows = out[jt * P : (jt + 1) * P, :]
+            half = C // 2
+            nc.scalar.activation(out=o[:, 0:half], in_=f[:, 0:half], func=ACT.Copy, scale=size_cols[:, jt : jt + 1])
+            if split_store:
+                nc.sync.dma_start(out=rows[:, 0:half], in_=o[:, 0:half])
+            nc.vector.tensor_scalar(
+                out=o[:, half:C], in0=f[:, half:C], scalar1=size_cols[:, jt : jt + 1], scalar2=None, op0=ALU.mult
+            )
+            if split_store:
+                nc.sync.dma_start(out=rows[:, half:C], in_=o[:, half:C])
             else:
-                nc.vector.tensor_scalar(
-                    out=o[:], in0=f_bank[jt][:, c0:c1], scalar1=size_cols[:, jt : jt + 1], scalar2=None, op0=ALU.mult
-                )
-            nc.sync.dma_start(out=out[jt * P : (jt + 1) * P, c0:c1], in_=o[:])
+                nc.sync.dma_start(out=rows, in_=o[:])
 
         nc.scalar.activation(out=warm_out[:], in_=warm[:], func=ACT.Ln)
         nc.scalar.activation(out=ln_a[:], in_=a_in[:].rearrange("p g t -> p (g t)"), func=ACT.Ln)
         nc.scalar.activation(out=warm_out[:], in_=warm[:], func=ACT.Exp)
 
-        sc_banks = [bank("u"), bank("u")]
+        sc_banks = [bank(), bank()]
         for c in range(8):
             nc.tensor.transpose(
                 sc_banks[c // 4][:, (c % 4) * P : (c % 4 + 1) * P],
@@ -270,102 +281,90 @@ def tile_huff_retail_flows_s3_kernel(
                 xs_wide[:].rearrange("p (n c) -> p n c", c=8)[:, :, 4 * i : 4 * i + 4],
                 sc_banks[i][:].rearrange("p (c n) -> p n c", c=4),
             )
-        size_bank = bank("u")
-        nc.tensor.transpose(size_bank[:, 0:P], size_rows32[:], ident[:])
-        group4("v", w_grp[0][:], w_raw[0][:])
-        zb = [turn_z(0, 0), turn_z(0, 1)]
-        empty_z(0, 0, zb[0], "s")
-        empty_z(0, 1, zb[1], "s")
-        quant_w(0)
+
+        def w_part(engine, h, c0, c1):
+            group4(engine, w_grp[h][:, c0:c1, :], w_raw[h][:, :, c0:c1])
+
+        w_part("v", 0, 0, 256)
+        w_part("s", 0, 256, 512)
+        zb = {}
+        xb = {}
+        zb[0] = turn_z(0)
+        zb[1] = turn_z(1)
+        empty_z(0, zb[0], "s")
+        empty_z(1, zb[1], "s")
         widen(0)
-        quant_z(0)
-        b0 = turn_x(0)
-        empty_x(0, b0, "s")
+        xb[0] = turn_x(0)
+        empty_x(0, xb[0], "s")
         widen(1)
-        b1 = turn_x(1)
-        for c in range(2):
-            cs = slice(c * 256, (c + 1) * 256)
-            group4("s", w_grp[1][:, cs, :], w_raw[1][:, :, cs])
-            if c == 0:
-                empty_x(1, b1, "s")
-        quant_x(0)
-        u_pass(0, 0, 0)
-        u_pass(1, 0, 0)
-        u_pass(0, 0, 1)
-        u_pass(0, 0, 2)
-        attract(0, 0)
+        xb[1] = turn_x(1)
+        w_part("s", 1, 0, 256)
+        empty_x(1, xb[1], "s")
         widen(2)
-        quant_x(1)
-        u_pass(1, 0, 1)
-        u_pass(1, 0, 2)
-        attract(1, 0)
-        quant_w(1)
-        u_group(0, 1)
-        attract(0, 1)
-        u_group(1, 1)
-        attract(1, 1)
+        zb[2] = turn_z(2)
+        xb[2] = turn_x(2)
+        quant_w(0)
+        quant_z(0)
+        quant_x(0)
+        empty_z(2, zb[2], "s")
+        w_part("s", 1, 256, 512)
+        empty_x(2, xb[2], "s")
         widen(3)
+        zb[3] = turn_z(3)
+        xb[3] = turn_x(3)
+        empty_z(3, zb[3], "s")
+        empty_x(3, xb[3], "s")
+        quant_x(1)
+        quant_w(1)
+        quant_z(1)
+        quant_x(2)
+        size_bank = bank()
+        nc.tensor.transpose(size_bank[:, 0:P], size_rows32[:], ident[:])
         nc.vector.tensor_copy(out=size_cols[:], in_=size_bank[:, 0:8])
+        widen(4)
+        quant_x(3)
+        quant_z(2)
+        widen(5)
+        quant_z(3)
 
-        p_work = {}
-        for g in range(3):
-            p_work[2 * g + 2] = (g, 0)
-            p_work[2 * g + 3] = (g, 1)
-        for n in range(0, 8):
-            nxt = n + 1
-            banks = []
-            if nxt < 8:
-                banks.append((turn_x(2 * nxt), "x", 2 * nxt))
-                banks.append((turn_x(2 * nxt + 1), "x", 2 * nxt + 1))
-                gz, hz = divmod(nxt + 1, 2)
-                if gz < G:
-                    banks.append((turn_z(gz, hz), "z", (gz, hz)))
-            groups = [] if n == 0 else [(2 * n, 0), (2 * n, 1), (2 * n + 1, 0), (2 * n + 1, 1)]
-            if n == 7:
-                groups = [(14, 0), (15, 0), (14, 1), (15, 1)]
-
-            def empty_one():
-                if banks:
-                    b, kind, which = banks.pop(0)
-                    if kind == "x":
-                        empty_x(which, b, "s")
-                    else:
-                        empty_z(which[0], which[1], b, "s")
-
-            if 2 * n + 4 < NT:
-                widen(2 * n + 4)
-            if n in p_work:
-                group_p(*p_work[n])
-            empty_one()
-            empty_one()
-            if nxt < 8:
-                quant_x(2 * nxt)
-            for m in range(2):
-                if m < len(groups):
-                    u_group(*groups[m])
-                    attract(*groups[m])
-                if m == 0:
-                    empty_one()
-            if 2 * n + 5 < NT:
-                widen(2 * n + 5)
-            if nxt < 8:
-                quant_x(2 * nxt + 1)
-                gz, hz = divmod(nxt + 1, 2)
-                if hz == 1 and gz < G:
-                    quant_z(gz)
-            if n in p_work:
-                quant_p(*p_work[n])
-            if n == 7:
-                u_group(*groups[2])
-                group_p(3, 0)
-                attract(*groups[2])
-                u_group(*groups[3])
-                attract(*groups[3])
+        p_first = {2: (0, 0), 3: (0, 1), 4: (1, 0), 5: (1, 1)}
+        order = {n: [(2 * n, 0), (2 * n, 1), (2 * n + 1, 0), (2 * n + 1, 1)] for n in range(8)}
+        order[0] = [(0, 0), (1, 0), (0, 1), (1, 1)]
+        order[6] = [(12, 0), (13, 0), (12, 1)]
+        order[7] = [(14, 0), (15, 0), (13, 1), (14, 1), (15, 1)]
+        for n in range(8):
+            for m, grp in enumerate(order[n]):
+                u_group(*grp)
+                attract(*grp)
+                if n == 7 and m == 1:
+                    group_p(3, 0)
+            xx, zz = n + 2, n + 4
+            if zz < 8:
+                bz = turn_z(zz)
+                empty_z(zz, bz, "s")
+            if xx < 8:
+                bx0 = turn_x(2 * xx)
+                bx1 = turn_x(2 * xx + 1)
+                empty_x(2 * xx, bx0, "s")
+                empty_x(2 * xx + 1, bx1, "s")
+                if 2 * xx + 2 < NT:
+                    widen(2 * xx + 2)
+                if n in p_first:
+                    group_p(*p_first[n])
+                if zz < 8:
+                    quant_z(zz)
+                quant_x(2 * xx)
+                if 2 * xx + 3 < NT:
+                    widen(2 * xx + 3)
+                quant_x(2 * xx + 1)
+                if n in p_first:
+                    quant_p(*p_first[n])
+            elif n == 6:
+                group_p(2, 0)
+                quant_p(2, 0)
+                group_p(2, 1)
             else:
-                for m in range(2, 4):
-                    if m < len(groups):
-                        u_group(*groups[m])
-                        attract(*groups[m])
+                quant_p(2, 1)
 
         for jt in range(3):
             for g in range(3):
@@ -374,12 +373,11 @@ def tile_huff_retail_flows_s3_kernel(
         group_p(3, 1)
         for g in range(3):
             f_pass(3, g)
+        quant_p(3, 1)
         for jt in range(4):
             f_pass(jt, 3)
-            finish(jt, "s", 0, 512)
-        quant_p(3, 1)
+            finish(jt, False)
         for jt in range(4, 8):
             for g in range(4):
                 f_pass(jt, g)
-            finish(jt, "s", 0, 256)
-            finish(jt, "v", 256, 512)
+            finish(jt, jt == 7)

@@ -107,17 +107,17 @@ def tile_huff_retail_flows_s3_kernel(
         nc.gpsimd.tensor_copy(out=size_rows32[:], in_=size_rows[:])
 
         load_x(0, 0, 2)
-        load_w(0)
         load_z(0, 0, 2)
-        load_x(0, 2, 4)
+        load_w(0)
         load_z(0, 2, 4)
-        load_scales(v_sc, v_scales, 2)
-        load_v(0)
+        load_x(0, 2, 4)
         load_w(1)
         load_z(1, 0, 2)
-        load_x(1, 0, 2)
-        load_v(1)
+        load_scales(v_sc, v_scales, 2)
+        load_v(0)
         load_z(1, 2, 4)
+        load_v(1)
+        load_x(1, 0, 2)
         load_x(1, 2, 4)
         for g in range(2, G):
             load_z(g, 0, 4)
@@ -126,7 +126,7 @@ def tile_huff_retail_flows_s3_kernel(
         nc.sync.dma_start(out=y_sb[:], in_=y_words.rearrange("g p n -> p g n"))
 
         def widen(i):
-            x_bf[i] = work.tile([P, K], BF16, name="x_bf", tag="x_bf", bufs=6, align_bytes=64)
+            x_bf[i] = work.tile([P, K], BF16, name="x_bf", tag="x_bf", bufs=8, align_bytes=64)
             t = i % 4
             nc.vector.tensor_tensor(
                 out=x_bf[i][:],
@@ -153,7 +153,7 @@ def tile_huff_retail_flows_s3_kernel(
                 nc.vector.tensor_copy(out=dst, in_=src)
 
         def empty_x(i, b, engine):
-            x_grp[i] = work.tile([P, 8 * P], BF16, name="x_grp", tag="x_grp", bufs=4, align_bytes=64)
+            x_grp[i] = work.tile([P, 8 * P], BF16, name="x_grp", tag="x_grp", bufs=6, align_bytes=64)
             dst = x_grp[i][:].bitcast(F32).rearrange("p (k h u) -> p k h u", k=2, u=2)
             copy_out(engine, dst, b[:].rearrange("p (k u h) -> p k h u", k=2, u=2))
 
@@ -168,11 +168,24 @@ def tile_huff_retail_flows_s3_kernel(
             b = bank()
             g, half = divmod(n, 2)
             for j in range(2):
-                words = z_raw[g][:, 2 * half + j, :].bitcast(F32)
                 for u in range(2):
                     c = 2 * j + u
-                    nc.tensor.transpose(b[:, c * P : (c + 1) * P], words[:, u:256:2], ident[:])
+                    if n in z_split:
+                        words = z_split[n][:].bitcast(F32)[:, c * P : (c + 1) * P]
+                    else:
+                        words = z_raw[g][:, 2 * half + j, :].bitcast(F32)[:, u:256:2]
+                    nc.tensor.transpose(b[:, c * P : (c + 1) * P], words, ident[:])
             return b
+
+        z_split = {}
+
+        def split_z(n):
+            g, half = divmod(n, 2)
+            z_split[n] = work.tile([P, 2 * D], BF16, name="z_split", tag="z_split", bufs=2, align_bytes=64)
+            nc.scalar.copy(
+                out=z_split[n][:].bitcast(F32).rearrange("p (t u w) -> p t u w", t=2, u=2),
+                in_=z_raw[g][:, 2 * half : 2 * half + 2, :].bitcast(F32).rearrange("p t (w u) -> p t u w", u=2),
+            )
 
         def empty_z(n, b, engine):
             z_grp[n] = work.tile([P, 8 * P], BF16, name="z_grp", tag="z_grp", bufs=4, align_bytes=64)
@@ -285,55 +298,65 @@ def tile_huff_retail_flows_s3_kernel(
         def w_part(engine, h, c0, c1):
             group4(engine, w_grp[h][:, c0:c1, :], w_raw[h][:, :, c0:c1])
 
-        w_part("v", 0, 0, 256)
-        w_part("s", 0, 256, 512)
         zb = {}
         xb = {}
-        zb[0] = turn_z(0)
-        zb[1] = turn_z(1)
-        empty_z(0, zb[0], "s")
-        empty_z(1, zb[1], "s")
         widen(0)
+        zb[0] = turn_z(0)
+        empty_z(0, zb[0], "s")
+        widen(1)
+        w_part("s", 0, 256, 512)
+        zb[1] = turn_z(1)
+        empty_z(1, zb[1], "s")
         xb[0] = turn_x(0)
         empty_x(0, xb[0], "s")
-        widen(1)
+        widen(2)
         xb[1] = turn_x(1)
         w_part("s", 1, 0, 256)
         empty_x(1, xb[1], "s")
-        widen(2)
+        w_part("v", 0, 0, 256)
         zb[2] = turn_z(2)
         xb[2] = turn_x(2)
+        widen(3)
+        w_part("s", 1, 256, 512)
+        empty_z(2, zb[2], "s")
+        split_z(4)
+        empty_x(2, xb[2], "s")
         quant_w(0)
         quant_z(0)
         quant_x(0)
-        empty_z(2, zb[2], "s")
-        w_part("s", 1, 256, 512)
-        empty_x(2, xb[2], "s")
-        widen(3)
+        quant_x(1)
+        quant_w(1)
         zb[3] = turn_z(3)
         xb[3] = turn_x(3)
         empty_z(3, zb[3], "s")
         empty_x(3, xb[3], "s")
-        quant_x(1)
-        quant_w(1)
-        quant_z(1)
-        quant_x(2)
+        widen(4)
+        widen(5)
         size_bank = bank()
         nc.tensor.transpose(size_bank[:, 0:P], size_rows32[:], ident[:])
         nc.vector.tensor_copy(out=size_cols[:], in_=size_bank[:, 0:8])
-        widen(4)
+        quant_z(1)
+        quant_x(2)
         quant_x(3)
-        quant_z(2)
-        widen(5)
-        quant_z(3)
 
-        p_first = {2: (0, 0), 3: (0, 1), 4: (1, 0), 5: (1, 1)}
+        p_work = {2:["I00"],3:["I01","Q00"],4:["I10","Q01"],5:["I11","Q10"],6:["Q11","I20","I21","Q20"],7:["Q21"]}
+
+        def do_p(work_list):
+            for it in work_list:
+                (group_p if it[0] == "I" else quant_p)(int(it[1]), int(it[2]))
+
         order = {n: [(2 * n, 0), (2 * n, 1), (2 * n + 1, 0), (2 * n + 1, 1)] for n in range(8)}
         order[0] = [(0, 0), (1, 0), (0, 1), (1, 1)]
         order[6] = [(12, 0), (13, 0), (12, 1)]
         order[7] = [(14, 0), (15, 0), (13, 1), (14, 1), (15, 1)]
         for n in range(8):
+            if 1 <= n <= 6:
+                quant_z(n + 1)
+                quant_x(2 * n + 2)
+                quant_x(2 * n + 3)
             for m, grp in enumerate(order[n]):
+                if m == 3 and n + 5 < 8:
+                    split_z(n + 5)
                 u_group(*grp)
                 attract(*grp)
                 if n == 7 and m == 1:
@@ -347,24 +370,10 @@ def tile_huff_retail_flows_s3_kernel(
                 bx1 = turn_x(2 * xx + 1)
                 empty_x(2 * xx, bx0, "s")
                 empty_x(2 * xx + 1, bx1, "s")
-                if 2 * xx + 2 < NT:
-                    widen(2 * xx + 2)
-                if n in p_first:
-                    group_p(*p_first[n])
-                if zz < 8:
-                    quant_z(zz)
-                quant_x(2 * xx)
-                if 2 * xx + 3 < NT:
-                    widen(2 * xx + 3)
-                quant_x(2 * xx + 1)
-                if n in p_first:
-                    quant_p(*p_first[n])
-            elif n == 6:
-                group_p(2, 0)
-                quant_p(2, 0)
-                group_p(2, 1)
-            else:
-                quant_p(2, 1)
+                for i in (2 * xx + 2, 2 * xx + 3):
+                    if i < NT:
+                        widen(i)
+            do_p(p_work.get(n, []))
 
         for jt in range(3):
             for g in range(3):

@@ -41,6 +41,7 @@ def tile_huff_retail_flows_s3_kernel(
 
         ident = kept("ident", [P, P], F32)
         warm = kept("warm", [P, 1], F32)
+        ones = kept("ones", [P, 512], BF16)
         warm_out = kept("warm_out", [P, 1], F32)
         a_in = kept("a_in", [P, G, 4], BF16)
         ln_a = kept("ln_a", [P, NT], F32)
@@ -53,7 +54,7 @@ def tile_huff_retail_flows_s3_kernel(
         v_sc = kept("v_sc", [P, 2 * J], U8)
         y_sb = kept("y_sb", [P, G, 2 * C], U8)
         y_sc = kept("y_sc", [P, G * C], U8)
-        w_raw = [kept("w_raw%d" % h, [P, 4, HALF], BF16) for h in range(2)]
+        w_raw = kept("w_raw", [P, 4, J], BF16)
         w_grp = [kept("w_grp%d" % h, [P, HALF, 4], BF16) for h in range(2)]
         w_q = [kept("w_q%d" % h, [P, HALF], U32) for h in range(2)]
         w_s = [kept("w_s%d" % h, [P, HALF], U8) for h in range(2)]
@@ -74,10 +75,8 @@ def tile_huff_retail_flows_s3_kernel(
         nc.scalar.dma_start(out=a_in[:], in_=a.rearrange("(g p t) -> p g t", p=P, t=4))
         nc.sync.dma_start(out=xs_cols[:], in_=x_scale.rearrange("o (p c) -> p (o c)", c=8))
 
-        w_view = w.rearrange("(p t) j -> p t j", t=4)
-
-        def load_w(h):
-            nc.sync.dma_start(out=w_raw[h][:], in_=w_view[:, :, h * HALF : (h + 1) * HALF])
+        def load_w():
+            nc.sync.dma_start(out=w_raw[:], in_=w.rearrange("(p t) j -> p t j", t=4))
 
         def load_z(g, t0, t1):
             src = z[512 * g : 512 * (g + 1), :].rearrange("(p t) k -> p t k", t=4)
@@ -87,9 +86,8 @@ def tile_huff_retail_flows_s3_kernel(
             src = x_bytes[512 * g : 512 * (g + 1), :].rearrange("(p t) k -> p (t k)", t=4)
             nc.sync.dma_start(out=x_raw[g][:, t0 * K : t1 * K], in_=src[:, t0 * K : t1 * K])
 
-        def load_v(h):
-            cs = slice(2 * HALF * h, 2 * HALF * (h + 1))
-            nc.sync.dma_start(out=v_sb[:, :, cs], in_=v_words.rearrange("g p n -> p g n")[:, :, cs])
+        def load_v():
+            nc.sync.dma_start(out=v_sb[:], in_=v_words.rearrange("g p n -> p g n"))
 
         def load_scales(tile, src, groups):
             for r in range(4):
@@ -98,25 +96,23 @@ def tile_huff_retail_flows_s3_kernel(
                     in_=src.bitcast(I32).rearrange("g (q r) n -> r q g n", r=4)[r],
                 )
 
-        nc.vector.memset(warm[:], 1.0)
         nc.vector.memset(v_sc[:].bitcast(I32), 0)
+        nc.vector.memset(warm[:], 1.0)
         nc.vector.memset(y_sc[:].bitcast(I32), 0)
-        make_identity(nc, ident[:])
         nc.gpsimd.memset(size_rows[:], 0.0)
-        nc.gpsimd.dma_start(out=size_rows[0:8, :], in_=size.rearrange("(c p) -> c p", p=P))
-        nc.gpsimd.tensor_copy(out=size_rows32[:], in_=size_rows[:])
+        nc.gpsimd.memset(ones[:], 1.0)
+        make_identity(nc, ident[:])
+        nc.scalar.dma_start(out=size_rows[0:8, :], in_=size.rearrange("(c p) -> c p", p=P))
 
         load_x(0, 0, 2)
         load_z(0, 0, 2)
-        load_w(0)
-        load_z(0, 2, 4)
+        load_w()
         load_x(0, 2, 4)
-        load_w(1)
+        load_z(0, 2, 4)
         load_z(1, 0, 2)
-        load_scales(v_sc, v_scales, 2)
-        load_v(0)
         load_z(1, 2, 4)
-        load_v(1)
+        load_scales(v_sc, v_scales, 2)
+        load_v()
         load_x(1, 0, 2)
         load_x(1, 2, 4)
         for g in range(2, G):
@@ -278,9 +274,12 @@ def tile_huff_retail_flows_s3_kernel(
                 nc.sync.dma_start(out=rows, in_=o[:])
 
         nc.scalar.activation(out=warm_out[:], in_=warm[:], func=ACT.Ln)
-        nc.scalar.activation(out=ln_a[:], in_=a_in[:].rearrange("p g t -> p (g t)"), func=ACT.Ln)
-        nc.scalar.activation(out=warm_out[:], in_=warm[:], func=ACT.Exp)
+        def keep_warm(count):
+            b = bank()
+            for k in range(count):
+                nc.tensor.matmul(out=b[:], lhsT=ones[:, 0:P], rhs=ones[:], start=True, stop=True)
 
+        keep_warm(2)
         sc_banks = [bank(), bank()]
         for c in range(8):
             nc.tensor.transpose(
@@ -295,49 +294,51 @@ def tile_huff_retail_flows_s3_kernel(
                 sc_banks[i][:].rearrange("p (c n) -> p n c", c=4),
             )
 
+        nc.scalar.activation(out=ln_a[:], in_=a_in[:].rearrange("p g t -> p (g t)"), func=ACT.Ln)
+        nc.scalar.activation(out=warm_out[:], in_=warm[:], func=ACT.Exp)
+
         def w_part(engine, h, c0, c1):
-            group4(engine, w_grp[h][:, c0:c1, :], w_raw[h][:, :, c0:c1])
+            group4(engine, w_grp[h][:, c0:c1, :], w_raw[:, :, h * HALF + c0 : h * HALF + c1])
 
         zb = {}
         xb = {}
         widen(0)
-        zb[0] = turn_z(0)
-        empty_z(0, zb[0], "s")
         widen(1)
-        w_part("s", 0, 256, 512)
-        zb[1] = turn_z(1)
-        empty_z(1, zb[1], "s")
-        xb[0] = turn_x(0)
-        empty_x(0, xb[0], "s")
         widen(2)
-        xb[1] = turn_x(1)
-        w_part("s", 1, 0, 256)
-        empty_x(1, xb[1], "s")
         w_part("v", 0, 0, 256)
-        zb[2] = turn_z(2)
-        xb[2] = turn_x(2)
         widen(3)
-        w_part("s", 1, 256, 512)
-        empty_z(2, zb[2], "s")
-        split_z(4)
-        empty_x(2, xb[2], "s")
+        for n in range(4):
+            if n < 2:
+                keep_warm(2 if n == 0 else 4)
+            zb[n] = turn_z(n)
+            if n == 0:
+                keep_warm(2)
+            xb[n] = turn_x(n)
+            if n == 2:
+                w_part("s", 1, 256, 512)
+            empty_z(n, zb[n], "s")
+            if n == 0:
+                w_part("s", 0, 256, 512)
+                w_part("s", 1, 0, 256)
+            empty_x(n, xb[n], "s")
         quant_w(0)
         quant_z(0)
         quant_x(0)
         quant_x(1)
         quant_w(1)
-        zb[3] = turn_z(3)
-        xb[3] = turn_x(3)
-        empty_z(3, zb[3], "s")
-        empty_x(3, xb[3], "s")
         widen(4)
         widen(5)
-        size_bank = bank()
-        nc.tensor.transpose(size_bank[:, 0:P], size_rows32[:], ident[:])
-        nc.vector.tensor_copy(out=size_cols[:], in_=size_bank[:, 0:8])
         quant_z(1)
         quant_x(2)
         quant_x(3)
+        keep_warm(1)
+        for h in range(2):
+            u_pass(0, h, 0)
+            u_pass(1, h, 0)
+            for i in range(2):
+                u_pass(i, h, 1)
+                u_pass(i, h, 2)
+                attract(i, h)
 
         p_work = {2:["I00"],3:["I01","Q00"],4:["I10","Q01"],5:["I11","Q10"],6:["Q11","I20","I21","Q20"],7:["Q21"]}
 
@@ -346,7 +347,7 @@ def tile_huff_retail_flows_s3_kernel(
                 (group_p if it[0] == "I" else quant_p)(int(it[1]), int(it[2]))
 
         order = {n: [(2 * n, 0), (2 * n, 1), (2 * n + 1, 0), (2 * n + 1, 1)] for n in range(8)}
-        order[0] = [(0, 0), (1, 0), (0, 1), (1, 1)]
+        order[0] = []
         order[6] = [(12, 0), (13, 0), (12, 1)]
         order[7] = [(14, 0), (15, 0), (13, 1), (14, 1), (15, 1)]
         for n in range(8):
@@ -355,24 +356,31 @@ def tile_huff_retail_flows_s3_kernel(
                 quant_x(2 * n + 2)
                 quant_x(2 * n + 3)
             for m, grp in enumerate(order[n]):
-                if m == 3 and n + 5 < 8:
-                    split_z(n + 5)
                 u_group(*grp)
                 attract(*grp)
+                if m == 0 and n + 4 < 8:
+                    split_z(n + 4)
                 if n == 7 and m == 1:
                     group_p(3, 0)
             xx, zz = n + 2, n + 4
-            if zz < 8:
-                bz = turn_z(zz)
-                empty_z(zz, bz, "s")
             if xx < 8:
                 bx0 = turn_x(2 * xx)
                 bx1 = turn_x(2 * xx + 1)
                 empty_x(2 * xx, bx0, "s")
                 empty_x(2 * xx + 1, bx1, "s")
+                if zz < 8:
+                    bz = turn_z(zz)
+                    empty_z(zz, bz, "s")
+                if xx == 7:
+                    size_bank = bank()
+                    nc.tensor.transpose(size_bank[:, 0:P], size_rows32[:], ident[:])
                 for i in (2 * xx + 2, 2 * xx + 3):
                     if i < NT:
                         widen(i)
+            if n == 3:
+                nc.scalar.copy(out=size_rows32[:], in_=size_rows[:])
+            if n == 6:
+                nc.vector.tensor_copy(out=size_cols[:], in_=size_bank[:, 0:8])
             do_p(p_work.get(n, []))
 
         for jt in range(3):

from contextlib import ExitStack

import concourse.mybir as mybir
from concourse.masks import make_identity

H, J, D, K, C = 2048, 1024, 512, 1024, 512
FLOPS = 2 * H * J * (D + K) + 2 * J * C * H

F32 = mybir.dt.float32
BF16 = mybir.dt.bfloat16
U32 = mybir.dt.uint32
I32 = mybir.dt.int32
U8 = mybir.dt.uint8
FP8 = mybir.dt.float8_e4m3fn
FP8X4 = mybir.dt.float8_e4m3fn_x4
FP4X4 = mybir.dt.float4_e2m1fn_x4
ACT = mybir.ActivationFunctionType
ALU = mybir.AluOpType

P = 128
G = H // 512
NT = 4 * G
HALF = J // 2


def tile_huff_retail_flows_s3_kernel(
    tc, z, w, x_bytes, x_scale, v_words, v_scales, a, size, y_words, y_scales, out
):
    nc = tc.nc
    with ExitStack() as ctx:
        keep = ctx.enter_context(tc.tile_pool(name="keep", bufs=1))
        work = ctx.enter_context(tc.tile_pool(name="work", bufs=2))
        psum = ctx.enter_context(tc.psum_pool(name="psum", bufs=1))
        ctx.enter_context(tc.manual_schedule())

        def kept(name, shape, dtype):
            return keep.tile(shape, dtype, name=name, tag=name, align_bytes=64)

        def bank():
            return psum.tile([P, 512], F32, name="bank", tag="bank", bufs=8)

        ident = kept("ident", [P, P], F32)
        warm = kept("warm", [P, 1], F32)
        ones = kept("ones", [P, 512], BF16)
        warm_out = kept("warm_out", [P, 1], F32)
        a_in = kept("a_in", [P, G, 4], BF16)
        ln_a = kept("ln_a", [P, NT], F32)
        xs_cols = kept("xs_cols", [P, 8], F32)
        xs_wide = kept("xs_wide", [P, K], F32)
        size_rows = kept("size_rows", [P, P], BF16)
        size_rows32 = kept("size_rows32", [P, P], F32)
        size_cols = kept("size_cols", [P, 8], F32)
        v_sb = kept("v_sb", [P, 2, 2 * J], U8)
        v_sc = kept("v_sc", [P, 2 * J], U8)
        y_sb = kept("y_sb", [P, G, 2 * C], U8)
        y_sc = kept("y_sc", [P, G * C], U8)
        w_raw = kept("w_raw", [P, 4, J], BF16)
        w_grp = [kept("w_grp%d" % h, [P, HALF, 4], BF16) for h in range(2)]
        w_q = [kept("w_q%d" % h, [P, HALF], U32) for h in range(2)]
        w_s = [kept("w_s%d" % h, [P, HALF], U8) for h in range(2)]
        z_raw = [kept("z_raw%d" % g, [P, 4, D], BF16) for g in range(G)]
        z_q = [kept("z_q%d" % n, [P, 256], U32) for n in range(2 * G)]
        z_s = [kept("z_s%d" % n, [P, 256], U8) for n in range(2 * G)]
        x_raw = [kept("x_raw%d" % g, [P, 4 * K], U8) for g in range(G)]
        x_q = [kept("x_q%d" % i, [P, 2, P], U32) for i in range(NT)]
        x_s = [kept("x_s%d" % i, [P, 2, P], U8) for i in range(NT)]
        p_q = [[kept("p_q%d_%d" % (g, h), [P, HALF], U32) for h in range(2)] for g in range(G)]
        p_s = [[kept("p_s%d_%d" % (g, h), [P, HALF], U8) for h in range(2)] for g in range(G)]
        z_grp = {}
        x_bf = {}
        x_grp = {}
        p_raw = {}
        p_grp = {}

        nc.scalar.dma_start(out=a_in[:], in_=a.rearrange("(g p t) -> p g t", p=P, t=4))
        nc.sync.dma_start(out=xs_cols[:], in_=x_scale.rearrange("o (p c) -> p (o c)", c=8))

        def load_w():
            nc.sync.dma_start(out=w_raw[:], in_=w.rearrange("(p t) j -> p t j", t=4))

        def load_z(g, t0, t1):
            src = z[512 * g : 512 * (g + 1), :].rearrange("(p t) k -> p t k", t=4)
            nc.sync.dma_start(out=z_raw[g][:, t0:t1, :], in_=src[:, t0:t1, :])

        def load_x(g, t0, t1):
            src = x_bytes[512 * g : 512 * (g + 1), :].rearrange("(p t) k -> p (t k)", t=4)
            nc.sync.dma_start(out=x_raw[g][:, t0 * K : t1 * K], in_=src[:, t0 * K : t1 * K])

        def load_v():
            nc.sync.dma_start(out=v_sb[:], in_=v_words.rearrange("g p n -> p g n"))

        def load_scales(tile, src, groups):
            for r in range(4):
                nc.sync.dma_start(
                    out=tile[r:P:32, :].bitcast(I32).rearrange("q (g n) -> q g n", g=groups),
                    in_=src.bitcast(I32).rearrange("g (q r) n -> r q g n", r=4)[r],
                )

        nc.vector.memset(v_sc[:].bitcast(I32), 0)
        nc.vector.memset(warm[:], 1.0)
        nc.vector.memset(y_sc[:].bitcast(I32), 0)
        nc.gpsimd.memset(size_rows[:], 0.0)
        nc.gpsimd.memset(ones[:], 1.0)
        make_identity(nc, ident[:])
        nc.scalar.dma_start(out=size_rows[0:8, :], in_=size.rearrange("(c p) -> c p", p=P))

        load_x(0, 0, 2)
        load_z(0, 0, 2)
        load_w()
        load_x(0, 2, 4)
        load_z(0, 2, 4)
        load_z(1, 0, 2)
        load_z(1, 2, 4)
        load_scales(v_sc, v_scales, 2)
        load_v()
        load_x(1, 0, 2)
        load_x(1, 2, 4)
        for g in range(2, G):
            load_z(g, 0, 4)
            load_x(g, 0, 4)
        load_scales(y_sc, y_scales, G)
        nc.sync.dma_start(out=y_sb[:], in_=y_words.rearrange("g p n -> p g n"))

        def widen(i):
            x_bf[i] = work.tile([P, K], BF16, name="x_bf", tag="x_bf", bufs=8, align_bytes=64)
            t = i % 4
            nc.vector.tensor_tensor(
                out=x_bf[i][:],
                in0=x_raw[i // 4][:, t * K : (t + 1) * K].bitcast(FP8),
                in1=xs_wide[:],
                op=ALU.mult,
            )

        def turn_x(i):
            b = bank()
            words = x_bf[i][:].bitcast(F32)
            for kg in range(2):
                for u in range(2):
                    c = 2 * kg + u
                    nc.tensor.transpose(
                        b[:, c * P : (c + 1) * P], words[:, 256 * kg + u : 256 * (kg + 1) : 2], ident[:]
                    )
            return b

        def copy_out(engine, dst, src):
            if engine == "s":
                nc.scalar.copy(out=dst, in_=src)
            else:
                nc.vector.tensor_copy(out=dst, in_=src)

        def empty_x(i, b, engine):
            x_grp[i] = work.tile([P, 8 * P], BF16, name="x_grp", tag="x_grp", bufs=6, align_bytes=64)
            dst = x_grp[i][:].bitcast(F32).rearrange("p (k h u) -> p k h u", k=2, u=2)
            copy_out(engine, dst, b[:].rearrange("p (k u h) -> p k h u", k=2, u=2))

        def quant_x(i):
            nc.vector.quantize_mx(
                out=x_q[i][:].rearrange("p k h -> p (k h)").bitcast(FP8X4),
                scales=x_s[i][:].rearrange("p k h -> p (k h)"),
                in_=x_grp[i][:],
            )

        def turn_z(n):
            b = bank()
            g, half = divmod(n, 2)
            for j in range(2):
                for u in range(2):
                    c = 2 * j + u
                    if n in z_split:
                        words = z_split[n][:].bitcast(F32)[:, c * P : (c + 1) * P]
                    else:
                        words = z_raw[g][:, 2 * half + j, :].bitcast(F32)[:, u:256:2]
                    nc.tensor.transpose(b[:, c * P : (c + 1) * P], words, ident[:])
            return b

        z_split = {}

        def split_z(n):
            g, half = divmod(n, 2)
            z_split[n] = work.tile([P, 2 * D], BF16, name="z_split", tag="z_split", bufs=2, align_bytes=64)
            nc.scalar.copy(
                out=z_split[n][:].bitcast(F32).rearrange("p (t u w) -> p t u w", t=2, u=2),
                in_=z_raw[g][:, 2 * half : 2 * half + 2, :].bitcast(F32).rearrange("p t (w u) -> p t u w", u=2),
            )

        def empty_z(n, b, engine):
            z_grp[n] = work.tile([P, 8 * P], BF16, name="z_grp", tag="z_grp", bufs=4, align_bytes=64)
            dst = z_grp[n][:].bitcast(F32).rearrange("p (t h u) -> p t h u", t=2, u=2)
            copy_out(engine, dst, b[:].rearrange("p (t u h) -> p t h u", t=2, u=2))

        def quant_z(n):
            nc.vector.quantize_mx(out=z_q[n][:].bitcast(FP8X4), scales=z_s[n][:], in_=z_grp[n][:])

        def group4(engine, dst, src):
            copy_out(
                engine, dst.rearrange("p (c i) t -> p c t i", i=4), src.rearrange("p t (c i) -> p c t i", i=4)
            )

        def quant_w(h):
            nc.vector.quantize_mx(
                out=w_q[h][:].bitcast(FP8X4), scales=w_s[h][:], in_=w_grp[h][:].rearrange("p n t -> p (n t)")
            )

        u_bank = {}

        def u_pass(i, h, which):
            if which == 0:
                u_bank[i, h] = bank()
            n, t = divmod(i, 2)
            cols = slice(t * P, (t + 1) * P)
            if which == 0:
                lhs, lsc = z_q[n][:, cols].bitcast(FP8X4), z_s[n][:, cols]
                rhs, rsc = w_q[h][:].bitcast(FP8X4), w_s[h][:]
            else:
                kg = which - 1
                lhs, lsc = x_q[i][:, kg, :].bitcast(FP8X4), x_s[i][:, kg, :]
                rhs = v_sb[:, kg, 2 * HALF * h : 2 * HALF * (h + 1)].bitcast(FP4X4)
                rsc = v_sc[:, J * kg + HALF * h : J * kg + HALF * (h + 1)]
            nc.tensor.matmul_mx(
                out=u_bank[i, h][:], lhsT=lhs, lhsT_scale=lsc, rhs=rhs, rhs_scale=rsc,
                start=(which == 0), stop=(which == 2),
            )

        def u_group(i, h):
            for which in range(3):
                u_pass(i, h, which)

        def attract(i, h):
            g, t = divmod(i, 4)
            if t == 0:
                p_raw[g, h] = work.tile([P, 4, HALF], BF16, name="p_raw", tag="p_raw", bufs=6, align_bytes=64)
            nc.scalar.activation(
                out=p_raw[g, h][:, t, :], in_=u_bank[i, h][:], func=ACT.Exp, bias=ln_a[:, i : i + 1], scale=1.0
            )

        def group_p(g, h):
            p_grp[g, h] = work.tile([P, HALF, 4], BF16, name="p_grp", tag="p_grp", bufs=2, align_bytes=64)
            group4("v", p_grp[g, h][:], p_raw[g, h][:])

        def quant_p(g, h):
            nc.vector.quantize_mx(
                out=p_q[g][h][:].bitcast(FP8X4), scales=p_s[g][h][:],
                in_=p_grp[g, h][:].rearrange("p n t -> p (n t)"),
            )

        f_bank = {}

        def f_pass(jt, g):
            if g == 0:
                f_bank[jt] = bank()
            h, c = divmod(jt, 4)
            cols = slice(c * P, (c + 1) * P)
            nc.tensor.matmul_mx(
                out=f_bank[jt][:],
                lhsT=p_q[g][h][:, cols].bitcast(FP8X4), lhsT_scale=p_s[g][h][:, cols],
                rhs=y_sb[:, g, :].bitcast(FP4X4), rhs_scale=y_sc[:, C * g : C * (g + 1)],
                start=(g == 0), stop=(g == G - 1),
            )

        def finish(jt, split_store):
            o = work.tile([P, C], F32, name="o_sb", tag="o_sb", bufs=8, align_bytes=64)
            f = f_bank[jt]
            rows = out[jt * P : (jt + 1) * P, :]
            half = C // 2
            nc.scalar.activation(out=o[:, 0:half], in_=f[:, 0:half], func=ACT.Copy, scale=size_cols[:, jt : jt + 1])
            if split_store:
                nc.sync.dma_start(out=rows[:, 0:half], in_=o[:, 0:half])
            nc.vector.tensor_scalar(
                out=o[:, half:C], in0=f[:, half:C], scalar1=size_cols[:, jt : jt + 1], scalar2=None, op0=ALU.mult
            )
            if split_store:
                nc.sync.dma_start(out=rows[:, half:C], in_=o[:, half:C])
            else:
                nc.sync.dma_start(out=rows, in_=o[:])

        nc.scalar.activation(out=warm_out[:], in_=warm[:], func=ACT.Ln)
        def keep_warm(count):
            b = bank()
            for k in range(count):
                nc.tensor.matmul(out=b[:], lhsT=ones[:, 0:P], rhs=ones[:], start=True, stop=True)

        keep_warm(2)
        sc_banks = [bank(), bank()]
        for c in range(8):
            nc.tensor.transpose(
                sc_banks[c // 4][:, (c % 4) * P : (c % 4 + 1) * P],
                xs_cols[:, c : c + 1].to_broadcast([P, P]),
                ident[:],
            )
        for i in range(2):
            copy_out(
                "vs"[i],
                xs_wide[:].rearrange("p (n c) -> p n c", c=8)[:, :, 4 * i : 4 * i + 4],
                sc_banks[i][:].rearrange("p (c n) -> p n c", c=4),
            )

        nc.scalar.activation(out=ln_a[:], in_=a_in[:].rearrange("p g t -> p (g t)"), func=ACT.Ln)
        nc.scalar.activation(out=warm_out[:], in_=warm[:], func=ACT.Exp)

        def w_part(engine, h, c0, c1):
            group4(engine, w_grp[h][:, c0:c1, :], w_raw[:, :, h * HALF + c0 : h * HALF + c1])

        zb = {}
        xb = {}
        widen(0)
        widen(1)
        widen(2)
        w_part("v", 0, 0, 256)
        widen(3)
        for n in range(4):
            if n < 2:
                keep_warm(2 if n == 0 else 4)
            zb[n] = turn_z(n)
            if n == 0:
                keep_warm(2)
            xb[n] = turn_x(n)
            if n == 2:
                w_part("s", 1, 256, 512)
            empty_z(n, zb[n], "s")
            if n == 0:
                w_part("s", 0, 256, 512)
                w_part("s", 1, 0, 256)
            empty_x(n, xb[n], "s")
        quant_w(0)
        quant_z(0)
        quant_x(0)
        quant_x(1)
        quant_w(1)
        widen(4)
        widen(5)
        quant_z(1)
        quant_x(2)
        quant_x(3)
        keep_warm(1)
        for h in range(2):
            u_pass(0, h, 0)
            u_pass(1, h, 0)
            for i in range(2):
                u_pass(i, h, 1)
                u_pass(i, h, 2)
                attract(i, h)

        p_work = {2:["I00"],3:["I01","Q00"],4:["I10","Q01"],5:["I11","Q10"],6:["Q11","I20","I21","Q20"],7:["Q21"]}

        def do_p(work_list):
            for it in work_list:
                (group_p if it[0] == "I" else quant_p)(int(it[1]), int(it[2]))

        order = {n: [(2 * n, 0), (2 * n, 1), (2 * n + 1, 0), (2 * n + 1, 1)] for n in range(8)}
        order[0] = []
        order[6] = [(12, 0), (13, 0), (12, 1)]
        order[7] = [(14, 0), (15, 0), (13, 1), (14, 1), (15, 1)]
        for n in range(8):
            if 1 <= n <= 6:
                quant_z(n + 1)
                quant_x(2 * n + 2)
                quant_x(2 * n + 3)
            for m, grp in enumerate(order[n]):
                u_group(*grp)
                attract(*grp)
                if m == 0 and n + 4 < 8:
                    split_z(n + 4)
                if n == 7 and m == 1:
                    group_p(3, 0)
            xx, zz = n + 2, n + 4
            if xx < 8:
                bx0 = turn_x(2 * xx)
                bx1 = turn_x(2 * xx + 1)
                empty_x(2 * xx, bx0, "s")
                empty_x(2 * xx + 1, bx1, "s")
                if zz < 8:
                    bz = turn_z(zz)
                    empty_z(zz, bz, "s")
                if xx == 7:
                    size_bank = bank()
                    nc.tensor.transpose(size_bank[:, 0:P], size_rows32[:], ident[:])
                for i in (2 * xx + 2, 2 * xx + 3):
                    if i < NT:
                        widen(i)
            if n == 3:
                nc.scalar.copy(out=size_rows32[:], in_=size_rows[:])
            if n == 6:
                nc.vector.tensor_copy(out=size_cols[:], in_=size_bank[:, 0:8])
            do_p(p_work.get(n, []))

        for jt in range(3):
            for g in range(3):
                f_pass(jt, g)
        quant_p(3, 0)
        group_p(3, 1)
        for g in range(3):
            f_pass(3, g)
        quant_p(3, 1)
        for jt in range(4):
            f_pass(jt, 3)
            finish(jt, False)
        for jt in range(4, 8):
            for g in range(4):
                f_pass(jt, g)
            finish(jt, jt == 7)
